import numpy as np
CORES = [61,69,101,62,70,102]
N = 6
F = 128
def setup_inputs(rng):
    return {"gr": rng.standard_normal((N, 128, F), dtype=np.float32) * (0.5 + np.abs(rng.standard_normal((1, 128, 1), dtype=np.float32))) * (0.5 + np.abs(rng.standard_normal((N, 1, F), dtype=np.float32)))}
def setup_inputs_big(rng):
    d = setup_inputs(rng)
    for k in ("gr",): d[k] = (d[k].astype(np.float32) * 1024.0).astype(d[k].dtype)
    return d
def setup_inputs_small(rng):
    d = setup_inputs(rng)
    for k in ("gr",): d[k] = (d[k].astype(np.float32) * (1 / 1024.0)).astype(d[k].dtype)
    return d
def setup_inputs_apart(rng):
    d = setup_inputs(rng)
    f = (10.0 ** rng.permutation(np.linspace(-1.5, 1.5, N))).astype(np.float32).reshape(N, 1, 1)
    for k in ("gr",): d[k] = (d[k].astype(np.float32) * f).astype(d[k].dtype)
    return d
def setup_inputs_mixed(rng):
    d = setup_inputs(rng)
    f = (10.0 ** rng.uniform(-3, 3, (1, 128, 1)) * 10.0 ** rng.uniform(-3, 3, (N, 1, F))).astype(np.float32)
    for k in ("gr",): d[k] = (d[k].astype(np.float32) * f).astype(d[k].dtype)
    return d
def reference(gr):
    G = gr.astype(np.float64); G2 = G ** 2
    R = G2.sum(axis=(0, 2)).reshape(1, 128, 1) / (N * F)
    Cm = G2.sum(axis=1, keepdims=True) / 128
    M = R.sum() / 128
    return {"y": (G / np.sqrt(R * Cm / M)).astype(np.float32)}

@@ -1,0 +1,180 @@
+from concourse.bass import DstId, RemoteDMATransfer
+from concourse.mybir import AluOpType, AxisListType, ActivationFunctionType
+
+BLK = 4
+NR = 6
+LEAF_ENGINES = 8
+
+SCRATCH = {
+    "G": ("sbuf", [128, 128], "float32"),
+    "SQ": ("sbuf", [128, 128], "float32"),
+    "land": ("sbuf", [128, NR * BLK], "float32"),
+    "ones": ("sbuf", [128, 128], "float32"),
+    "ident": ("sbuf", [128, 128], "float32"),
+    "diag": ("sbuf", [128, 128], "float32"),
+    "Gc": ("sbuf", [128, 128], "float32"),
+    "Y": ("sbuf", [128, 128], "float32"),
+    "sc": ("sbuf", [128, 16], "float32"),
+    "csP": ("psum", [128, 512], "float32"),
+    "cbP": ("psum", [128, 512], "float32"),
+    "mP": ("psum", [128, 512], "float32"),
+}
+SEMAPHORES = ["ld", "st", "sib", "arr", "sent", "one_s", "pad_s", "id_s", "sq_s", "cs_s", "s0_s", "c0_s", "w_s", "v_s",
+              "dg_s", "cb_s", "gc_s", "rs_s", "m_s", "rr_s", "rn_s", "ms_s", "rm_s", "f0_s", "a_s", "b_s", "s2_s", "y_s"]
+
+
+def _engines(mask):
+    return [1 << b for b in range(16) if (mask >> b) & 1]
+
+
+def _join(bits):
+    m = 0
+    for b in bits:
+        m |= b
+    return m
+
+
+def _plan(T, topo):
+    chips = []
+    for c in T.cores:
+        if topo.chip(c) not in chips:
+            chips.append(topo.chip(c))
+    groups, col, base = [], {}, {}
+    nxt = 0
+    for ch in chips:
+        mem = [c for c in T.cores if topo.chip(c) == ch]
+        out = [c for c in T.cores if topo.chip(c) != ch]
+        fwd = [c for c in mem if all(topo.may_write(c, d) for d in out)][0]
+        leaves = [c for c in mem if c != fwd]
+        start = nxt
+        for c in leaves + [fwd]:
+            col[c] = nxt
+            nxt += BLK
+        for c in mem:
+            base[c] = (start, nxt)
+        groups.append((leaves, fwd, out))
+    return groups, col, base
+
+
+def rank_program(g, core, T, topo):
+    if T.rank_of(core) is None:
+        return
+    S = T.sem
+    A = ActivationFunctionType
+    mult, add = AluOpType.mult, AluOpType.add
+    groups, col, base = _plan(T, topo)
+    leaves, fwd, out = [gr for gr in groups if core in gr[0] or core == gr[1]][0]
+    own = col[core]
+    k = lambda i: T.sc[:, i:i + 1]
+    s0, c0, w, v, Rs, rR, Rn, Ms, rM, f0, a, b, s2 = [k(i) for i in range(13)]
+
+    def fwd_masks(f, dests):
+        m = topo.mask(f, dests[0])
+        for d in dests:
+            m &= topo.mask(f, d)
+        eng = _engines(m)
+        per = 1
+        while per * 2 * len(dests) <= len(eng):
+            per *= 2
+        return eng, per
+
+    g.sync.dma_start(T.G[:], T.gr[:]).then_inc(S.ld, 16)
+    g.vector.memset(T.land[:, own + 1:own + BLK], 0.0).then_inc(S.pad_s, 1)
+    g.vector.memset(T.ones[:], 1.0).then_inc(S.one_s, 1)
+    g.wait_ge(S.one_s, 1)
+    g.affine_select(T.ident[:], T.ones[:], [[-1, 128]], AluOpType.is_equal, 0.0, 0, 1).then_inc(S.id_s, 1)
+
+    g.scalar.wait_ge(S.ld, 16)
+    g.scalar.activation(T.SQ[:], T.G[:], A.Square, accum_out=T.land[:, own:own + 1]).then_inc(S.sq_s, 1)
+
+    g.wait_ge(S.pad_s, 1)
+    g.wait_ge(S.sq_s, 1)
+    blk = T.land[:, own:own + BLK]
+    sent = 0
+    if core != fwd:
+        rid, pid, _ = topo.addr(fwd)
+        m = _engines(topo.mask(core, fwd))[:LEAF_ENGINES]
+        g.remote_dma(out_ap=blk, in_ap=blk, remote_sem=S.sib, local_sem=S.sent, pid=pid, routing_id=rid,
+                     dma_engine_mask=_join(m))
+        sent += len(m)
+        eng, _p = fwd_masks(fwd, out)
+        sib_total = len(eng)
+    else:
+        eng, per = fwd_masks(core, out)
+        for lf in leaves:
+            rid, pid, _ = topo.addr(lf)
+            g.remote_dma(out_ap=blk, in_ap=blk, remote_sem=S.sib, local_sem=S.sent, pid=pid, routing_id=rid,
+                         dma_engine_mask=_join(eng) & topo.mask(core, lf))
+            sent += len(eng)
+        sib_total = LEAF_ENGINES * len(leaves)
+        g.wait_ge(S.sib, sib_total)
+        lo, hi = base[core]
+        piece = T.land[:, lo:hi]
+        trs = []
+        for i, d in enumerate(out):
+            rid, pid, _ = topo.addr(d)
+            trs.append(RemoteDMATransfer(dst_ids=[DstId(rid=rid, pnc=pid)],
+                                         dma_engine_mask=_join(eng[i * per:(i + 1) * per]),
+                                         remote_sem=S.arr, src=piece, dst=piece))
+            sent += per
+        g.remote_dma_fused(trs, local_sem=S.sent)
+    arr_total = 0
+    for (_l, f, o) in groups:
+        if core in o:
+            arr_total += fwd_masks(f, o)[1]
+
+    g.tensor.wait_ge(S.sq_s, 1)
+    g.tensor.wait_ge(S.one_s, 1)
+    g.tensor.matmul(T.csP[:, 0:1], T.SQ[:], T.ones[:, 0:1], True, True).then_inc(S.cs_s, 1)
+    g.scalar.wait_ge(S.cs_s, 1)
+    g.scalar.activation(s0, T.csP[:, 0:1], A.Sqrt).then_inc(S.s0_s, 1)
+    V = g.vector
+    V.wait_ge(S.s0_s, 1)
+    V.reciprocal(c0, s0).then_inc(S.c0_s, 1)
+    V.wait_ge(S.c0_s, 1)
+    V.tensor_scalar(w, c0, c0, T.csP[:, 0:1], mult, mult).then_inc(S.w_s, 1)
+    V.wait_ge(S.w_s, 1)
+    V.tensor_scalar(v, w, -0.75, 2.25, mult, add).then_inc(S.v_s, 1)
+    V.wait_ge(S.v_s, 1)
+    V.wait_ge(S.id_s, 1)
+    V.tensor_scalar(T.diag[:], T.ident[:], c0, v, mult, mult).then_inc(S.dg_s, 1)
+    g.tensor.wait_ge(S.dg_s, 1)
+    g.tensor.matmul(T.cbP[:, 0:128], T.ones[:], T.diag[:], True, True).then_inc(S.cb_s, 1)
+    V.wait_ge(S.cb_s, 1)
+    V.wait_ge(S.ld, 16)
+    V.tensor_tensor(T.Gc[:], T.G[:], T.cbP[:, 0:128], mult).then_inc(S.gc_s, 1)
+
+    V.wait_ge(S.gc_s, 1)
+    V.wait_ge(S.pad_s, 1)
+    V.wait_ge(S.sq_s, 1)
+    V.wait_ge(S.sib, sib_total)
+    V.wait_ge(S.arr, arr_total)
+    V.tensor_reduce(Rs, T.land[:], AxisListType.X, add).then_inc(S.rs_s, 1)
+    g.tensor.wait_ge(S.rs_s, 1)
+    g.tensor.matmul(T.mP[:, 0:1], T.ones[:], Rs, True, True).then_inc(S.m_s, 1)
+    V.wait_ge(S.rs_s, 1)
+    V.reciprocal(rR, Rs).then_inc(S.rr_s, 1)
+    g.scalar.wait_ge(S.rs_s, 1)
+    g.scalar.activation(Rn, Rs, A.Copy, scale=-1.0 / 3.0).then_inc(S.rn_s, 1)
+    V.wait_ge(S.m_s, 1)
+    V.tensor_copy(Ms, T.mP[:, 0:1]).then_inc(S.ms_s, 1)
+    V.wait_ge(S.ms_s, 1)
+    V.reciprocal(rM, Ms).then_inc(S.rm_s, 1)
+    g.scalar.wait_ge(S.ms_s, 1)
+    g.scalar.wait_ge(S.rr_s, 1)
+    g.scalar.activation(f0, Ms, A.Sqrt, scale=rR).then_inc(S.f0_s, 1)
+    g.scalar.wait_ge(S.f0_s, 1)
+    g.scalar.activation(a, f0, A.Square).then_inc(S.a_s, 1)
+    g.scalar.wait_ge(S.a_s, 1)
+    g.scalar.wait_ge(S.rn_s, 1)
+    g.scalar.activation(b, a, A.Identity, bias=Ms, scale=Rn).then_inc(S.b_s, 1)
+    g.scalar.wait_ge(S.b_s, 1)
+    g.scalar.activation(s2, b, A.Copy, scale=f0).then_inc(S.s2_s, 1)
+    V.wait_ge(S.rm_s, 1)
+    V.wait_ge(S.s2_s, 1)
+    V.tensor_scalar(T.Y[:], T.Gc[:], rM, s2, mult, mult).then_inc(S.y_s, 1)
+
+    g.sync.wait_ge(S.y_s, 1)
+    g.sync.dma_start(T.y[:], T.Y[:]).then_inc(S.st, 16)
+    g.sync.wait_ge(S.st, 16)
+    g.wait_ge(S.sent, sent)

@@ -1,26 +1,31 @@
 from concourse.bass import DstId, RemoteDMATransfer
 from concourse.mybir import AluOpType, AxisListType, ActivationFunctionType
 
-BLK = 4
-NR = 6
+REM = 4
+FB, LB = 4, 8
+FV, LV = 7, 8
+W = 12
 LEAF_ENGINES = 8
+H = 64
 
 SCRATCH = {
     "G": ("sbuf", [128, 128], "float32"),
     "SQ": ("sbuf", [128, 128], "float32"),
-    "land": ("sbuf", [128, NR * BLK], "float32"),
+    "land": ("sbuf", [128, W], "float32"),
     "ones": ("sbuf", [128, 128], "float32"),
     "ident": ("sbuf", [128, 128], "float32"),
+    "diagR": ("sbuf", [128, 128], "float32"),
     "diag": ("sbuf", [128, 128], "float32"),
     "Gc": ("sbuf", [128, 128], "float32"),
     "Y": ("sbuf", [128, 128], "float32"),
     "sc": ("sbuf", [128, 16], "float32"),
-    "csP": ("psum", [128, 512], "float32"),
+    "csA": ("psum", [128, 512], "float32"),
+    "csB": ("psum", [128, 512], "float32"),
     "cbP": ("psum", [128, 512], "float32"),
     "mP": ("psum", [128, 512], "float32"),
 }
-SEMAPHORES = ["ld", "st", "sib", "arr", "sent", "one_s", "pad_s", "id_s", "sq_s", "cs_s", "s0_s", "c0_s", "w_s", "v_s",
-              "dg_s", "cb_s", "gc_s", "rs_s", "m_s", "rr_s", "rn_s", "ms_s", "rm_s", "f0_s", "a_s", "b_s", "s2_s", "y_s"]
+SEMAPHORES = ["ld", "st", "sib", "arr", "sent", "one_s", "pad_s", "id_s", "sq_s", "csa_s", "csb_s", "s0_s", "rc_s",
+              "dr_s", "w_s", "v_s", "dg_s", "cb_s", "gc_s", "rs_s", "m_s", "rr_s", "f0_s", "y_s"]
 
 
 def _engines(mask):
@@ -39,21 +44,25 @@ def _plan(T, topo):
     for c in T.cores:
         if topo.chip(c) not in chips:
             chips.append(topo.chip(c))
-    groups, col, base = [], {}, {}
-    nxt = 0
+    groups = []
     for ch in chips:
         mem = [c for c in T.cores if topo.chip(c) == ch]
         out = [c for c in T.cores if topo.chip(c) != ch]
         fwd = [c for c in mem if all(topo.may_write(c, d) for d in out)][0]
-        leaves = [c for c in mem if c != fwd]
-        start = nxt
-        for c in leaves + [fwd]:
-            col[c] = nxt
-            nxt += BLK
-        for c in mem:
-            base[c] = (start, nxt)
-        groups.append((leaves, fwd, out))
-    return groups, col, base
+        leaf = [c for c in mem if c != fwd][0]
+        groups.append((leaf, fwd, out))
+    return groups
+
+
+def _fwd_engines(topo, f, dests):
+    m = topo.mask(f, dests[0])
+    for d in dests:
+        m &= topo.mask(f, d)
+    eng = _engines(m)
+    per = 1
+    while per * 2 * len(dests) <= len(eng):
+        per *= 2
+    return eng, per
 
 
 def rank_program(g, core, T, topo):
@@ -62,82 +71,83 @@ def rank_program(g, core, T, topo):
     S = T.sem
     A = ActivationFunctionType
     mult, add = AluOpType.mult, AluOpType.add
-    groups, col, base = _plan(T, topo)
-    leaves, fwd, out = [gr for gr in groups if core in gr[0] or core == gr[1]][0]
-    own = col[core]
+    groups = _plan(T, topo)
+    group_of = {}
+    for i, (lf, fw, _o) in enumerate(groups):
+        group_of[lf] = i
+        group_of[fw] = i
+    me = group_of[core]
+    leaf, fwd, out = groups[me]
+    is_fwd = core == fwd
     k = lambda i: T.sc[:, i:i + 1]
-    s0, c0, w, v, Rs, rR, Rn, Ms, rM, f0, a, b, s2 = [k(i) for i in range(13)]
+    s0, rC, w, v, Rs, rR, f0 = [k(i) for i in range(7)]
+    V = g.vector
 
-    def fwd_masks(f, dests):
-        m = topo.mask(f, dests[0])
-        for d in dests:
-            m &= topo.mask(f, d)
-        eng = _engines(m)
-        per = 1
-        while per * 2 * len(dests) <= len(eng):
-            per *= 2
-        return eng, per
+    if is_fwd:
+        val, pad, blk = T.land[:, FV:FV + 1], T.land[:, FB:FV], T.land[:, FB:FB + 4]
+    else:
+        val, pad, blk = T.land[:, LV:LV + 1], T.land[:, LV + 1:LB + 4], T.land[:, LB:LB + 4]
 
     g.sync.dma_start(T.G[:], T.gr[:]).then_inc(S.ld, 16)
-    g.vector.memset(T.land[:, own + 1:own + BLK], 0.0).then_inc(S.pad_s, 1)
-    g.vector.memset(T.ones[:], 1.0).then_inc(S.one_s, 1)
+    V.memset(pad, 0.0).then_inc(S.pad_s, 1)
+    V.memset(T.ones[:], 1.0).then_inc(S.one_s, 1)
     g.wait_ge(S.one_s, 1)
     g.affine_select(T.ident[:], T.ones[:], [[-1, 128]], AluOpType.is_equal, 0.0, 0, 1).then_inc(S.id_s, 1)
 
     g.scalar.wait_ge(S.ld, 16)
-    g.scalar.activation(T.SQ[:], T.G[:], A.Square, accum_out=T.land[:, own:own + 1]).then_inc(S.sq_s, 1)
+    g.scalar.activation(T.SQ[:], T.G[:], A.Square, accum_out=val).then_inc(S.sq_s, 1)
 
     g.wait_ge(S.pad_s, 1)
     g.wait_ge(S.sq_s, 1)
-    blk = T.land[:, own:own + BLK]
     sent = 0
-    if core != fwd:
+    eng, per = _fwd_engines(topo, fwd, out)
+    if not is_fwd:
         rid, pid, _ = topo.addr(fwd)
         m = _engines(topo.mask(core, fwd))[:LEAF_ENGINES]
         g.remote_dma(out_ap=blk, in_ap=blk, remote_sem=S.sib, local_sem=S.sent, pid=pid, routing_id=rid,
                      dma_engine_mask=_join(m))
         sent += len(m)
-        eng, _p = fwd_masks(fwd, out)
         sib_total = len(eng)
     else:
-        eng, per = fwd_masks(core, out)
-        for lf in leaves:
-            rid, pid, _ = topo.addr(lf)
-            g.remote_dma(out_ap=blk, in_ap=blk, remote_sem=S.sib, local_sem=S.sent, pid=pid, routing_id=rid,
-                         dma_engine_mask=_join(eng) & topo.mask(core, lf))
-            sent += len(eng)
-        sib_total = LEAF_ENGINES * len(leaves)
+        rid, pid, _ = topo.addr(leaf)
+        g.remote_dma(out_ap=blk, in_ap=blk, remote_sem=S.sib, local_sem=S.sent, pid=pid, routing_id=rid,
+                     dma_engine_mask=_join(eng) & topo.mask(core, leaf))
+        sent += len(eng)
+        sib_total = LEAF_ENGINES
         g.wait_ge(S.sib, sib_total)
-        lo, hi = base[core]
-        piece = T.land[:, lo:hi]
+        pair = T.land[:, FV:LV + 1]
         trs = []
         for i, d in enumerate(out):
             rid, pid, _ = topo.addr(d)
+            slot = [x for x in range(len(groups)) if x != group_of[d]].index(me)
             trs.append(RemoteDMATransfer(dst_ids=[DstId(rid=rid, pnc=pid)],
                                          dma_engine_mask=_join(eng[i * per:(i + 1) * per]),
-                                         remote_sem=S.arr, src=piece, dst=piece))
+                                         remote_sem=S.arr, src=pair, dst=T.land[:, 2 * slot:2 * slot + 2]))
             sent += per
         g.remote_dma_fused(trs, local_sem=S.sent)
     arr_total = 0
     for (_l, f, o) in groups:
         if core in o:
-            arr_total += fwd_masks(f, o)[1]
+            arr_total += _fwd_engines(topo, f, o)[1]
 
     g.tensor.wait_ge(S.sq_s, 1)
     g.tensor.wait_ge(S.one_s, 1)
-    g.tensor.matmul(T.csP[:, 0:1], T.SQ[:], T.ones[:, 0:1], True, True).then_inc(S.cs_s, 1)
-    g.scalar.wait_ge(S.cs_s, 1)
-    g.scalar.activation(s0, T.csP[:, 0:1], A.Sqrt).then_inc(S.s0_s, 1)
-    V = g.vector
-    V.wait_ge(S.s0_s, 1)
-    V.reciprocal(c0, s0).then_inc(S.c0_s, 1)
-    V.wait_ge(S.c0_s, 1)
-    V.tensor_scalar(w, c0, c0, T.csP[:, 0:1], mult, mult).then_inc(S.w_s, 1)
-    V.wait_ge(S.w_s, 1)
-    V.tensor_scalar(v, w, -0.75, 2.25, mult, add).then_inc(S.v_s, 1)
-    V.wait_ge(S.v_s, 1)
+    g.tensor.matmul(T.csA[:, 0:1], T.SQ[:], T.ones[:, 0:1], True, True).then_inc(S.csa_s, 1)
+    g.tensor.matmul(T.csB[:, 0:1], T.SQ[:], T.ones[:, 0:1], True, True).then_inc(S.csb_s, 1)
+    g.scalar.wait_ge(S.csa_s, 1)
+    g.scalar.activation(s0, T.csA[:, 0:1], A.Sqrt).then_inc(S.s0_s, 1)
+    V.wait_ge(S.csb_s, 1)
+    V.reciprocal(rC, T.csB[:, 0:1]).then_inc(S.rc_s, 1)
+    V.wait_ge(S.rc_s, 1)
     V.wait_ge(S.id_s, 1)
-    V.tensor_scalar(T.diag[:], T.ident[:], c0, v, mult, mult).then_inc(S.dg_s, 1)
+    V.tensor_scalar(T.diagR[:], T.ident[:], rC, None, mult).then_inc(S.dr_s, 1)
+    V.wait_ge(S.s0_s, 1)
+    V.tensor_scalar(w, s0, s0, rC, mult, mult).then_inc(S.w_s, 1)
+    V.wait_ge(S.w_s, 1)
+    V.tensor_scalar(v, w, -0.5, 1.5, mult, add).then_inc(S.v_s, 1)
+    V.wait_ge(S.v_s, 1)
+    V.wait_ge(S.dr_s, 1)
+    V.tensor_scalar(T.diag[:], T.diagR[:], s0, v, mult, mult).then_inc(S.dg_s, 1)
     g.tensor.wait_ge(S.dg_s, 1)
     g.tensor.matmul(T.cbP[:, 0:128], T.ones[:], T.diag[:], True, True).then_inc(S.cb_s, 1)
     V.wait_ge(S.cb_s, 1)
@@ -154,27 +164,16 @@ def rank_program(g, core, T, topo):
     g.tensor.matmul(T.mP[:, 0:1], T.ones[:], Rs, True, True).then_inc(S.m_s, 1)
     V.wait_ge(S.rs_s, 1)
     V.reciprocal(rR, Rs).then_inc(S.rr_s, 1)
-    g.scalar.wait_ge(S.rs_s, 1)
-    g.scalar.activation(Rn, Rs, A.Copy, scale=-1.0 / 3.0).then_inc(S.rn_s, 1)
-    V.wait_ge(S.m_s, 1)
-    V.tensor_copy(Ms, T.mP[:, 0:1]).then_inc(S.ms_s, 1)
-    V.wait_ge(S.ms_s, 1)
-    V.reciprocal(rM, Ms).then_inc(S.rm_s, 1)
-    g.scalar.wait_ge(S.ms_s, 1)
+    g.scalar.wait_ge(S.m_s, 1)
     g.scalar.wait_ge(S.rr_s, 1)
-    g.scalar.activation(f0, Ms, A.Sqrt, scale=rR).then_inc(S.f0_s, 1)
+    g.scalar.activation(f0, T.mP[:, 0:1], A.Sqrt, scale=rR).then_inc(S.f0_s, 1)
+    V.wait_ge(S.f0_s, 1)
+    V.tensor_scalar(T.Y[:, 0:H], T.Gc[:, 0:H], f0, None, mult).then_inc(S.y_s, 1)
     g.scalar.wait_ge(S.f0_s, 1)
-    g.scalar.activation(a, f0, A.Square).then_inc(S.a_s, 1)
-    g.scalar.wait_ge(S.a_s, 1)
-    g.scalar.wait_ge(S.rn_s, 1)
-    g.scalar.activation(b, a, A.Identity, bias=Ms, scale=Rn).then_inc(S.b_s, 1)
-    g.scalar.wait_ge(S.b_s, 1)
-    g.scalar.activation(s2, b, A.Copy, scale=f0).then_inc(S.s2_s, 1)
-    V.wait_ge(S.rm_s, 1)
-    V.wait_ge(S.s2_s, 1)
-    V.tensor_scalar(T.Y[:], T.Gc[:], rM, s2, mult, mult).then_inc(S.y_s, 1)
+    g.scalar.wait_ge(S.gc_s, 1)
+    g.scalar.activation(T.Y[:, H:128], T.Gc[:, H:128], A.Copy, scale=f0).then_inc(S.y_s, 1)
 
-    g.sync.wait_ge(S.y_s, 1)
+    g.sync.wait_ge(S.y_s, 2)
     g.sync.dma_start(T.y[:], T.Y[:]).then_inc(S.st, 16)
     g.sync.wait_ge(S.st, 16)
     g.wait_ge(S.sent, sent)

from concourse.bass import DstId, RemoteDMATransfer
from concourse.mybir import AluOpType, AxisListType, ActivationFunctionType

REM = 4
FB, LB = 4, 8
FV, LV = 7, 8
W = 12
LEAF_ENGINES = 8
H = 64

SCRATCH = {
    "G": ("sbuf", [128, 128], "float32"),
    "SQ": ("sbuf", [128, 128], "float32"),
    "land": ("sbuf", [128, W], "float32"),
    "ones": ("sbuf", [128, 128], "float32"),
    "ident": ("sbuf", [128, 128], "float32"),
    "diagR": ("sbuf", [128, 128], "float32"),
    "diag": ("sbuf", [128, 128], "float32"),
    "Gc": ("sbuf", [128, 128], "float32"),
    "Y": ("sbuf", [128, 128], "float32"),
    "sc": ("sbuf", [128, 16], "float32"),
    "csA": ("psum", [128, 512], "float32"),
    "csB": ("psum", [128, 512], "float32"),
    "cbP": ("psum", [128, 512], "float32"),
    "mP": ("psum", [128, 512], "float32"),
}
SEMAPHORES = ["ld", "st", "sib", "arr", "sent", "one_s", "pad_s", "id_s", "sq_s", "csa_s", "csb_s", "s0_s", "rc_s",
              "dr_s", "w_s", "v_s", "dg_s", "cb_s", "gc_s", "rs_s", "m_s", "rr_s", "f0_s", "y_s"]


def _engines(mask):
    return [1 << b for b in range(16) if (mask >> b) & 1]


def _join(bits):
    m = 0
    for b in bits:
        m |= b
    return m


def _plan(T, topo):
    chips = []
    for c in T.cores:
        if topo.chip(c) not in chips:
            chips.append(topo.chip(c))
    groups = []
    for ch in chips:
        mem = [c for c in T.cores if topo.chip(c) == ch]
        out = [c for c in T.cores if topo.chip(c) != ch]
        fwd = [c for c in mem if all(topo.may_write(c, d) for d in out)][0]
        leaf = [c for c in mem if c != fwd][0]
        groups.append((leaf, fwd, out))
    return groups


def _fwd_engines(topo, f, dests):
    m = topo.mask(f, dests[0])
    for d in dests:
        m &= topo.mask(f, d)
    eng = _engines(m)
    per = 1
    while per * 2 * len(dests) <= len(eng):
        per *= 2
    return eng, per


def rank_program(g, core, T, topo):
    if T.rank_of(core) is None:
        return
    S = T.sem
    A = ActivationFunctionType
    mult, add = AluOpType.mult, AluOpType.add
    groups = _plan(T, topo)
    group_of = {}
    for i, (lf, fw, _o) in enumerate(groups):
        group_of[lf] = i
        group_of[fw] = i
    me = group_of[core]
    leaf, fwd, out = groups[me]
    is_fwd = core == fwd
    k = lambda i: T.sc[:, i:i + 1]
    s0, rC, w, v, Rs, rR, f0 = [k(i) for i in range(7)]
    V = g.vector

    if is_fwd:
        val, pad, blk = T.land[:, FV:FV + 1], T.land[:, FB:FV], T.land[:, FB:FB + 4]
    else:
        val, pad, blk = T.land[:, LV:LV + 1], T.land[:, LV + 1:LB + 4], T.land[:, LB:LB + 4]

    g.sync.dma_start(T.G[:], T.gr[:]).then_inc(S.ld, 16)
    V.memset(pad, 0.0).then_inc(S.pad_s, 1)
    V.memset(T.ones[:], 1.0).then_inc(S.one_s, 1)
    g.wait_ge(S.one_s, 1)
    g.affine_select(T.ident[:], T.ones[:], [[-1, 128]], AluOpType.is_equal, 0.0, 0, 1).then_inc(S.id_s, 1)

    g.scalar.wait_ge(S.ld, 16)
    g.scalar.activation(T.SQ[:], T.G[:], A.Square, accum_out=val).then_inc(S.sq_s, 1)

    g.wait_ge(S.pad_s, 1)
    g.wait_ge(S.sq_s, 1)
    sent = 0
    eng, per = _fwd_engines(topo, fwd, out)
    if not is_fwd:
        rid, pid, _ = topo.addr(fwd)
        m = _engines(topo.mask(core, fwd))[:LEAF_ENGINES]
        g.remote_dma(out_ap=blk, in_ap=blk, remote_sem=S.sib, local_sem=S.sent, pid=pid, routing_id=rid,
                     dma_engine_mask=_join(m))
        sent += len(m)
        sib_total = len(eng)
    else:
        rid, pid, _ = topo.addr(leaf)
        g.remote_dma(out_ap=blk, in_ap=blk, remote_sem=S.sib, local_sem=S.sent, pid=pid, routing_id=rid,
                     dma_engine_mask=_join(eng) & topo.mask(core, leaf))
        sent += len(eng)
        sib_total = LEAF_ENGINES
        g.wait_ge(S.sib, sib_total)
        pair = T.land[:, FV:LV + 1]
        trs = []
        for i, d in enumerate(out):
            rid, pid, _ = topo.addr(d)
            slot = [x for x in range(len(groups)) if x != group_of[d]].index(me)
            trs.append(RemoteDMATransfer(dst_ids=[DstId(rid=rid, pnc=pid)],
                                         dma_engine_mask=_join(eng[i * per:(i + 1) * per]),
                                         remote_sem=S.arr, src=pair, dst=T.land[:, 2 * slot:2 * slot + 2]))
            sent += per
        g.remote_dma_fused(trs, local_sem=S.sent)
    arr_total = 0
    for (_l, f, o) in groups:
        if core in o:
            arr_total += _fwd_engines(topo, f, o)[1]

    g.tensor.wait_ge(S.sq_s, 1)
    g.tensor.wait_ge(S.one_s, 1)
    g.tensor.matmul(T.csA[:, 0:1], T.SQ[:], T.ones[:, 0:1], True, True).then_inc(S.csa_s, 1)
    g.tensor.matmul(T.csB[:, 0:1], T.SQ[:], T.ones[:, 0:1], True, True).then_inc(S.csb_s, 1)
    g.scalar.wait_ge(S.csa_s, 1)
    g.scalar.activation(s0, T.csA[:, 0:1], A.Sqrt).then_inc(S.s0_s, 1)
    V.wait_ge(S.csb_s, 1)
    V.reciprocal(rC, T.csB[:, 0:1]).then_inc(S.rc_s, 1)
    V.wait_ge(S.rc_s, 1)
    V.wait_ge(S.id_s, 1)
    V.tensor_scalar(T.diagR[:], T.ident[:], rC, None, mult).then_inc(S.dr_s, 1)
    V.wait_ge(S.s0_s, 1)
    V.tensor_scalar(w, s0, s0, rC, mult, mult).then_inc(S.w_s, 1)
    V.wait_ge(S.w_s, 1)
    V.tensor_scalar(v, w, -0.5, 1.5, mult, add).then_inc(S.v_s, 1)
    V.wait_ge(S.v_s, 1)
    V.wait_ge(S.dr_s, 1)
    V.tensor_scalar(T.diag[:], T.diagR[:], s0, v, mult, mult).then_inc(S.dg_s, 1)
    g.tensor.wait_ge(S.dg_s, 1)
    g.tensor.matmul(T.cbP[:, 0:128], T.ones[:], T.diag[:], True, True).then_inc(S.cb_s, 1)
    V.wait_ge(S.cb_s, 1)
    V.wait_ge(S.ld, 16)
    V.tensor_tensor(T.Gc[:], T.G[:], T.cbP[:, 0:128], mult).then_inc(S.gc_s, 1)

    V.wait_ge(S.gc_s, 1)
    V.wait_ge(S.pad_s, 1)
    V.wait_ge(S.sq_s, 1)
    V.wait_ge(S.sib, sib_total)
    V.wait_ge(S.arr, arr_total)
    V.tensor_reduce(Rs, T.land[:], AxisListType.X, add).then_inc(S.rs_s, 1)
    g.tensor.wait_ge(S.rs_s, 1)
    g.tensor.matmul(T.mP[:, 0:1], T.ones[:], Rs, True, True).then_inc(S.m_s, 1)
    V.wait_ge(S.rs_s, 1)
    V.reciprocal(rR, Rs).then_inc(S.rr_s, 1)
    g.scalar.wait_ge(S.m_s, 1)
    g.scalar.wait_ge(S.rr_s, 1)
    g.scalar.activation(f0, T.mP[:, 0:1], A.Sqrt, scale=rR).then_inc(S.f0_s, 1)
    V.wait_ge(S.f0_s, 1)
    V.tensor_scalar(T.Y[:, 0:H], T.Gc[:, 0:H], f0, None, mult).then_inc(S.y_s, 1)
    g.scalar.wait_ge(S.f0_s, 1)
    g.scalar.wait_ge(S.gc_s, 1)
    g.scalar.activation(T.Y[:, H:128], T.Gc[:, H:128], A.Copy, scale=f0).then_inc(S.y_s, 1)

    g.sync.wait_ge(S.y_s, 2)
    g.sync.dma_start(T.y[:], T.Y[:]).then_inc(S.st, 16)
    g.sync.wait_ge(S.st, 16)
    g.wait_ge(S.sent, sent)
